import numpy as np
import ml_dtypes


def mxq(x, axis, fmt="e4m3"):
    dtype, down = {"e4m3": (ml_dtypes.float8_e4m3fn, 7), "e5m2": (ml_dtypes.float8_e5m2, 14)}[fmt]
    v = np.moveaxis(np.asarray(x, np.float32).astype(ml_dtypes.bfloat16).astype(np.float64), axis, -1)
    blocks = v.reshape(v.shape[:-1] + (-1, 32))
    amax = np.abs(blocks).max(-1, keepdims=True)
    byte = np.maximum(np.where(amax > 0, np.frexp(amax)[1] - 1 + 127, 0) - down, 1)
    scale = np.exp2(byte - 127.0)
    codes = (blocks / scale).astype(np.float32).astype(dtype).astype(np.float64)
    return np.moveaxis((codes * scale).reshape(v.shape), -1, axis)


WIDE = False


def mx_kscale(k):
    if not WIDE:
        return np.ones(k)
    levels = np.array([10, -10, 5, -5, 0])
    if k % 512:
        return np.exp2(np.random.permutation(np.resize(levels, k // 32))).repeat(32)
    a = np.empty((k // 512, 16))
    for p in range(k // 512):
        a[p, :8] = np.random.permutation(np.resize(levels, 8))
        for g in range(8):
            far = levels[np.abs(levels - a[p, g]) >= 10]
            a[p, g + 8] = far[np.random.randint(len(far))]
    return np.exp2(a.ravel()).repeat(32)


def f64(x):
    return np.asarray(x).astype(np.float64)


def striped(idx):
    return np.tile(np.asarray(idx).reshape(-1, 16).T, (8, 1)).astype(np.uint16)


def unstriped(offs):
    return offs[:16].T.reshape(-1).astype(np.int64)


E2M1 = np.array([0.0, 0.5, 1.0, 1.5, 2.0, 3.0, 4.0, 6.0, -0.0, -0.5, -1.0, -1.5, -2.0, -3.0, -4.0, -6.0])


def pack_weight(w, fmt):
    k, n = w.shape
    w = f64(np.asarray(w, np.float32).astype(ml_dtypes.bfloat16)).reshape(k // 32, 32, n)
    amax = np.abs(w).max(1)
    if fmt == "e4m3":
        byte = np.frexp(amax)[1] - 1 + 127 - 7
    else:
        mant, ex = np.frexp(amax / 6.0)
        byte = np.where(mant > 0.5, ex, ex - 1) + 127
    byte = np.clip(np.where(amax > 0, byte, 1), 1, 254)
    scaled = (w * np.exp2(127.0 - byte)[:, None, :]).reshape(k, n).astype(np.float32)
    by_word = np.ascontiguousarray(scaled.reshape(k // 512, 128, 4, n).transpose(0, 1, 3, 2))
    if fmt == "e4m3":
        words = by_word.astype(ml_dtypes.float8_e4m3fn).view(np.uint8)
    else:
        c = by_word.astype(ml_dtypes.float4_e2m1fn).view(np.uint8) & 0xF
        words = (c[..., 0::2] | (c[..., 1::2] << 4)).reshape(k // 512, 128, 2 * n)
    return np.ascontiguousarray(words), np.ascontiguousarray(byte.astype(np.uint8).reshape(k // 512, 16, n))


def unpack_weight(words, scales, fmt):
    g, _, n = scales.shape
    words = np.ascontiguousarray(words).reshape(g, 128, n, -1)
    if fmt == "e4m3":
        vals = words.view(ml_dtypes.float8_e4m3fn).astype(np.float64)
    else:
        nib = np.empty((g, 128, n, 4), np.uint8)
        nib[..., 0::2] = words & 0xF
        nib[..., 1::2] = words >> 4
        vals = E2M1[nib]
    vals = vals * np.repeat(np.exp2(scales.astype(np.float64) - 127.0), 8, axis=1)[..., None]
    return vals.transpose(0, 1, 3, 2).reshape(g * 512, n)


D, E, T, I, Q, G = 512, 512, 2048, 512, 128, 32


def setup_inputs():
    n = np.random.standard_normal
    idx = np.random.permutation(T)[:I]
    fd = mx_kscale(D)
    fi = mx_kscale(I)
    ti = np.ones(T)
    ti[idx] = fi
    keysp = pack_weight(n((D, T)) / fd[:, None], "e2m1")
    return {
        "query": (n((D, Q)) * 0.8 / np.sqrt(D) * fd[:, None]).astype(np.float32),
        "keys_words": keysp[0],
        "keys_scales": keysp[1],
        "dquery": (n((D, Q)) * 0.6 / np.sqrt(D) * fd[:, None]).astype(np.float32),
        "os": (np.random.uniform(4.0, 16.0, (1, I)) * fi).astype(np.float32),
        "vals": (n((E, T)) / ti).astype(np.float32),
        "offs": striped(idx),
    }


def reference(query, keys_words, keys_scales, dquery, os, vals, offs):
    idx = unstriped(offs)
    keysu = unpack_weight(keys_words, keys_scales, "e2m1")
    queryq = mxq(f64(query), 0, "e4m3")
    keysidxg = keysu[:, idx]
    a = queryq.T @ keysidxg
    dqueryq = mxq(f64(dquery), 0, "e4m3")
    ta = dqueryq.T @ keysidxg
    m1 = a.reshape(Q, G, I // G).mean(axis=2)
    mr = np.repeat(m1, I // G, axis=1)
    ce = a - mr
    v1 = np.sqrt(np.square(ce).reshape(Q, G, I // G).mean(axis=2) + 0.3)
    vr = np.repeat(v1, I // G, axis=1)
    s = ce / vr
    p = np.exp(s - np.max(s, axis=1, keepdims=True))
    z = np.sum(p, axis=1, keepdims=True)
    tm1 = ta.reshape(Q, G, I // G).mean(axis=2)
    tmr = np.repeat(tm1, I // G, axis=1)
    tce = ta - tmr
    tv1 = (tce * ce * 2.0).reshape(Q, G, I // G).mean(axis=2) * 0.5 / v1
    tvr = np.repeat(tv1, I // G, axis=1)
    ts = (tce - tvr * ce / vr) / vr
    tp = ts * p
    tz = np.sum(tp, axis=1, keepdims=True)
    tw = (tp - tz * p / z) / z
    wo1 = tw * f64(os)
    wt1 = wo1.T
    vt1 = f64(vals)[:, idx].T
    wt1q = mxq(wt1, 0, "e4m3")
    vt1q = mxq(vt1, 0, "e4m3")
    o = wt1q.T @ vt1q
    return o

@@ -1,0 +1,272 @@
+from contextlib import ExitStack
+
+import concourse.mybir as mybir
+from concourse.masks import make_identity
+
+D, E, T, I, Q, G = 512, 512, 2048, 512, 128, 32
+FLOPS = 2 * Q * I * (2 * D + E)
+
+F32 = mybir.dt.float32
+BF16 = mybir.dt.bfloat16
+I32 = mybir.dt.int32
+U32 = mybir.dt.uint32
+U16 = mybir.dt.uint16
+U8 = mybir.dt.uint8
+FP8X4 = mybir.dt.float8_e4m3fn_x4
+FP4X4 = mybir.dt.float4_e2m1fn_x4
+ALU = mybir.AluOpType
+ACT = mybir.ActivationFunctionType
+AX = mybir.AxisListType
+
+P = 128
+PACK = 4
+PAGE = I // G
+E_BLOCKS = E // P
+SCALAR_BLOCKS = (0, 3)
+CAST_COLS = 512
+OUT_COLS = 256
+
+
+def tile_attend_ttpagestandard_kernel(tc, query, keys_words, keys_scales, dquery, slot_factor, vals, offs, out):
+    nc = tc.nc
+    with ExitStack() as ctx:
+        sb = ctx.enter_context(tc.tile_pool(name="sb", bufs=1))
+        ps = ctx.enter_context(tc.psum_pool(name="ps", bufs=1))
+
+        def paged(ap):
+            return ap.rearrange("p (g j) -> p g j", j=PAGE)
+
+        def per_slot(ap):
+            return ap.unsqueeze(2).to_broadcast([P, G, PAGE])
+
+        offsets = sb.tile([P, I // 16], U16, name="offsets")
+        nc.sync.dma_start(offsets[:], offs)
+        ks_pool = sb.tile([P, T], U8, name="ks_pool", align_bytes=64)
+        nc.gpsimd.memset(ks_pool[:].bitcast(I32), 0)
+        for quad in range(4):
+            nc.scalar.dma_start(
+                ks_pool[32 * quad : 32 * quad + 4, :].bitcast(I32),
+                keys_scales[0, 4 * quad : 4 * quad + 4, :].bitcast(I32),
+            )
+
+        def load_rows(src, name):
+            raw = sb.tile([P, PACK, Q], F32, name=name)
+            nc.sync.dma_start(raw[:], src.rearrange("(p j) w -> p j w", j=PACK))
+            return raw
+
+        q_raw = load_rows(query, "q_raw")
+        kw_pool = sb.tile([P, T], U16, name="kw_pool", align_bytes=64)
+        nc.sync.dma_start(kw_pool[:].bitcast(I32), keys_words[0].bitcast(I32))
+        dq_raw = load_rows(dquery, "dq_raw")
+        v_pool = {}
+
+        def load_values(b, part, parts):
+            width = T // parts
+            name = "v_pool%d_%d" % (b, part)
+            v_pool[b, part] = sb.tile([P, width], F32, name=name, tag=name, align_bytes=64)
+            nc.sync.dma_start(v_pool[b, part][:], vals[b * P : (b + 1) * P, part * width : (part + 1) * width])
+
+        load_values(0, 0, 2)
+        load_values(0, 1, 2)
+        os_cols = sb.tile([P, PACK], F32, name="os_cols")
+        nc.sync.dma_start(os_cols[:], slot_factor.rearrange("o (p t) -> (o p) t", t=PACK))
+        load_values(1, 0, 1)
+        load_values(3, 0, 2)
+        load_values(2, 0, 1)
+        load_values(3, 1, 2)
+
+        ident = sb.tile([P, P], F32, name="ident")
+        make_identity(nc, ident[:])
+
+        warm_in = sb.tile([P, 1], F32, name="warm_in")
+        warm_out = sb.tile([P, 1], F32, name="warm_out")
+        nc.gpsimd.memset(warm_in[:], 1.0)
+        nc.scalar.activation(warm_out[:], warm_in[:], ACT.Abs_reciprocal_sqrt)
+
+        ks = sb.tile([P, I], U8, name="ks", align_bytes=64)
+        nc.vector.tensor_copy(ks[:], ks_pool[:].indirect(offsets[:]))
+
+        def quantize_rows(raw, name):
+            grouped = sb.tile([P, Q * PACK], BF16, name=name + "_grouped", align_bytes=64)
+            nc.scalar.copy(grouped[:].rearrange("p (w j) -> p w j", j=PACK), raw[:].rearrange("p j w -> p w j"))
+            codes = sb.tile([P, Q], U32, name=name + "_codes", align_bytes=64)
+            scales = sb.tile([P, Q], U8, name=name + "_scales", align_bytes=64)
+            nc.vector.quantize_mx(out=codes[:].bitcast(FP8X4), scales=scales[:], in_=grouped[:])
+            return codes, scales
+
+        q_mx = quantize_rows(q_raw, "q")
+        kw = []
+        for h in range(2):
+            half = sb.tile([P, I // 2], U16, name="kw%d" % h, align_bytes=64)
+            nc.vector.tensor_copy(half[:], kw_pool[:].indirect(offsets[:, 16 * h : 16 * (h + 1)]))
+            kw.append(half)
+        dq_mx = quantize_rows(dq_raw, "dq")
+
+        scores = []
+        for n, (codes, scales) in enumerate((q_mx, dq_mx)):
+            bank = ps.tile([P, I], F32, name="scores%d" % n)
+            for h in range(2):
+                cols = slice(h * I // 2, (h + 1) * I // 2)
+                nc.tensor.matmul_mx(
+                    out=bank[:, cols],
+                    lhsT=codes[:].bitcast(FP8X4),
+                    lhsT_scale=scales[:],
+                    rhs=kw[h][:].bitcast(FP4X4),
+                    rhs_scale=ks[:, cols],
+                    start=True,
+                    stop=True,
+                )
+            scores.append(bank)
+        a, ta = scores
+
+        os_bank = ps.tile([P, PACK, P], F32, name="os_bank")
+        for t in range(PACK):
+            nc.tensor.transpose(os_bank[:, t, :], os_cols[:, t : t + 1].to_broadcast([P, P]), ident[:])
+
+
+        def turn(word_sets, dst_words, tag, copy):
+            bank = ps.tile([P, 2, P], F32, name=tag, tag=tag)
+            for u in range(2):
+                nc.tensor.transpose(bank[:, u, :], word_sets[u], ident[:])
+            copy(dst_words.rearrange("p (r u) -> p r u", u=2), bank[:].rearrange("p u r -> p r u"))
+
+        rounded = {}
+        picked = {}
+
+        def round_values(b, part):
+            if part == 0:
+                rounded[b] = sb.tile([P, T], BF16, name="rounded%d" % b, tag="rounded%d" % b, align_bytes=64)
+            for c in range(0, T // 2, CAST_COLS):
+                c0 = part * T // 2 + c
+                nc.scalar.activation(rounded[b][:, c0 : c0 + CAST_COLS], v_pool[b, part][:, c : c + CAST_COLS], ACT.Copy)
+
+        def gather_values(b, tag):
+            picked[b] = sb.tile([P, I], BF16, name="picked%d" % b, tag=tag, align_bytes=64)
+            if b in SCALAR_BLOCKS:
+                nc.scalar.activation(picked[b][:], rounded[b][:].indirect(offsets[:]), ACT.Copy)
+            else:
+                nc.vector.tensor_copy(picked[b][:], v_pool[b, 0][:].indirect(offsets[:]))
+
+        def turn_values(b):
+            words = picked[b][:].bitcast(F32)
+            turn([words[:, u : 2 * P : 2] for u in range(2)], v_grouped[b // 2][:].bitcast(F32)[:, 2 * P * (b % 2) : 2 * P * (b % 2 + 1)], "turn%d" % b, nc.scalar.copy)
+
+        def big(name, tag=None):
+            return sb.tile([P, I], F32, name=name, tag=tag or name, align_bytes=64)
+
+        def small(name, tag=None):
+            return sb.tile([P, G], F32, name=name, tag=tag or name, align_bytes=64)
+
+        def column(name):
+            return sb.tile([P, 1], F32, name=name)
+
+        a_sum, ta_sum = small("a_sum"), small("ta_sum")
+        nc.vector.tensor_reduce(a_sum[:], paged(a[:]), AX.X, ALU.add)
+        nc.vector.tensor_reduce(ta_sum[:], paged(ta[:]), AX.X, ALU.add)
+        ce, tce = big("ce"), big("tce")
+        nc.vector.scalar_tensor_tensor(paged(ce[:]), per_slot(a_sum[:]), -1.0 / PAGE, paged(a[:]), ALU.mult, ALU.add)
+        nc.vector.scalar_tensor_tensor(paged(tce[:]), per_slot(ta_sum[:]), -1.0 / PAGE, paged(ta[:]), ALU.mult, ALU.add)
+        round_values(0, 0)
+        round_values(0, 1)
+        gather_values(0, "picked0")
+        sq = big("sq", "rounded0")
+        nc.scalar.activation(sq[:], ce[:], ACT.Square)
+        round_values(3, 0)
+        cross = big("cross")
+        nc.vector.tensor_tensor(cross[:], ta[:], ce[:], ALU.mult)
+        sq_sum, cross_sum = small("sq_sum"), small("cross_sum")
+        nc.vector.tensor_reduce(sq_sum[:], paged(sq[:]), AX.X, ALU.add)
+        nc.vector.tensor_reduce(cross_sum[:], paged(cross[:]), AX.X, ALU.add)
+        r, r2 = small("r", "v_pool3_0"), small("r2")
+        nc.scalar.activation(r[:], sq_sum[:], ACT.Abs_reciprocal_sqrt, bias=0.3, scale=1.0 / PAGE)
+        nc.scalar.activation(r2[:], r[:], ACT.Square, scale=0.25)
+        warm_exp = column("warm_exp")
+        nc.scalar.activation(warm_exp[:], r2[:, 0:1], ACT.Exp, scale=-1.0)
+
+        gather_values(1, "rounded0")
+        k = small("k")
+        nc.vector.tensor_tensor(k[:], cross_sum[:], r2[:], ALU.mult)
+        s = big("s")
+        nc.vector.tensor_tensor(paged(s[:]), paged(ce[:]), per_slot(r[:]), ALU.mult)
+        x = big("x")
+        nc.vector.tensor_tensor(paged(x[:]), paged(tce[:]), per_slot(r[:]), ALU.mult)
+        y = big("y")
+        nc.vector.tensor_tensor(paged(y[:]), paged(s[:]), per_slot(k[:]), ALU.mult)
+        neg_max = column("neg_max")
+        nc.vector.tensor_reduce(neg_max[:], s[:], AX.X, ALU.max, negate=True)
+        round_values(3, 1)
+        p, z = big("p", "v_pool3_1"), column("z")
+        nc.scalar.activation(p[:], s[:], ACT.Exp, bias=neg_max[:], accum_out=z[:])
+        gather_values(3, "picked3")
+        ts = big("ts")
+        nc.vector.tensor_tensor(ts[:], x[:], y[:], ALU.subtract)
+        gather_values(2, "ce")
+
+        v_grouped = [
+            sb.tile([P, OUT_COLS * PACK], BF16, name="v_grouped%d" % h, tag=("sq_sum", "v_grouped1")[h], align_bytes=64)
+            for h in range(2)
+        ]
+        for b in (0, 1, 2, 3):
+            turn_values(b)
+        v_mx = []
+
+        def quantize_values(h, tag):
+            v_codes = sb.tile([P, OUT_COLS], U32, name="v_codes%d" % h, tag=tag, align_bytes=64)
+            v_scales = sb.tile([P, OUT_COLS], U8, name="v_scales%d" % h, align_bytes=64)
+            nc.vector.quantize_mx(out=v_codes[:].bitcast(FP8X4), scales=v_scales[:], in_=v_grouped[h][:])
+            v_mx.append((v_codes, v_scales))
+
+        rz = column("rz")
+        nc.vector.reciprocal(rz[:], z[:])
+        tp, tz, tau = big("tp"), column("tz"), column("tau")
+        nc.vector.scalar_tensor_tensor(tp[:], p[:], 1.0, ts[:], ALU.mult, ALU.mult, accum_out=tz[:])
+        pos = big("pos")
+        nc.vector.scalar_tensor_tensor(
+            pos[:].rearrange("p (n t) -> p n t", t=PACK),
+            p[:].rearrange("p (n t) -> p n t", t=PACK),
+            rz[:],
+            os_bank[:].rearrange("p t n -> p n t"),
+            ALU.mult,
+            ALU.mult,
+        )
+        nc.vector.tensor_tensor(tau[:], tz[:], rz[:], ALU.mult)
+        quantize_values(0, "tp")
+        w = []
+        for u in range(2):
+            part = sb.tile([P, P, 2], BF16, name="w%d" % u, align_bytes=64)
+            nc.vector.scalar_tensor_tensor(
+                part[:],
+                ts[:].rearrange("p (n t) -> p n t", t=PACK)[:, :, 2 * u : 2 * u + 2],
+                tau[:],
+                pos[:].rearrange("p (n t) -> p n t", t=PACK)[:, :, 2 * u : 2 * u + 2],
+                ALU.subtract,
+                ALU.mult,
+            )
+            w.append(part[:].rearrange("p n e -> p (n e)").bitcast(F32))
+        w_grouped = sb.tile([P, Q * PACK], BF16, name="w_grouped", align_bytes=64)
+        turn(w, w_grouped[:].bitcast(F32), "turn_w", nc.vector.tensor_copy)
+        w_codes = sb.tile([P, Q], U32, name="w_codes", align_bytes=64)
+        w_scales = sb.tile([P, Q], U8, name="w_scales", align_bytes=64)
+        nc.vector.quantize_mx(out=w_codes[:].bitcast(FP8X4), scales=w_scales[:], in_=w_grouped[:])
+
+        quantize_values(1, "pos")
+
+        for h in range(E // OUT_COLS):
+            cols = slice(h * OUT_COLS, (h + 1) * OUT_COLS)
+            acc = ps.tile([P, OUT_COLS], F32, name="acc%d" % h, tag="scores%d" % h)
+            nc.tensor.matmul_mx(
+                out=acc[:],
+                lhsT=w_codes[:].bitcast(FP8X4),
+                lhsT_scale=w_scales[:],
+                rhs=v_mx[h][0][:].bitcast(FP8X4),
+                rhs_scale=v_mx[h][1][:],
+                start=True,
+                stop=True,
+            )
+            res = sb.tile([P, OUT_COLS], F32, name="res%d" % h)
+            if h == 0:
+                nc.scalar.copy(res[:], acc[:])
+                nc.scalar.dma_start(out[:, cols], res[:])
+            else:
+                nc.vector.tensor_copy(res[:], acc[:])
+                nc.sync.dma_start(out[:, cols], res[:])

@@ -68,9 +68,9 @@ def tile_attend_ttpagestandard_kernel(tc, query, keys_words, keys_scales, dquery
 
         load_values(0, 0, 2)
         load_values(0, 1, 2)
-        os_cols = sb.tile([P, PACK], F32, name="os_cols")
-        nc.sync.dma_start(os_cols[:], slot_factor.rearrange("o (p t) -> (o p) t", t=PACK))
         load_values(1, 0, 1)
+        os_cols = sb.tile([P, PACK], F32, name="os_cols", tag="os_cols", align_bytes=64)
+        nc.sync.dma_start(os_cols[:], slot_factor.rearrange("o (p t) -> (o p) t", t=PACK))
         load_values(3, 0, 2)
         load_values(2, 0, 1)
         load_values(3, 1, 2)
@@ -81,6 +81,8 @@ def tile_attend_ttpagestandard_kernel(tc, query, keys_words, keys_scales, dquery
         warm_in = sb.tile([P, 1], F32, name="warm_in")
         warm_out = sb.tile([P, 1], F32, name="warm_out")
         nc.gpsimd.memset(warm_in[:], 1.0)
+        zero = sb.tile([P, 1], F32, name="zero", tag="zero", align_bytes=64)
+        nc.gpsimd.memset(zero[:], 0.0)
         nc.scalar.activation(warm_out[:], warm_in[:], ACT.Abs_reciprocal_sqrt)
 
         ks = sb.tile([P, I], U8, name="ks", align_bytes=64)
@@ -169,12 +171,13 @@ def tile_attend_ttpagestandard_kernel(tc, query, keys_words, keys_scales, dquery
         round_values(0, 0)
         round_values(0, 1)
         gather_values(0, "picked0")
-        sq = big("sq", "rounded0")
-        nc.scalar.activation(sq[:], ce[:], ACT.Square)
+        gather_values(1, "picked1")
+        sq = big("sq", "os_cols")
+        nc.scalar.activation(sq[:], ce[:], ACT.Square, bias=zero[:])
         round_values(3, 0)
         cross = big("cross")
-        nc.vector.tensor_tensor(cross[:], ta[:], ce[:], ALU.mult)
-        sq_sum, cross_sum = small("sq_sum"), small("cross_sum")
+        nc.gpsimd.tensor_tensor(cross[:], tce[:], ce[:], ALU.mult)
+        sq_sum, cross_sum = small("sq_sum"), small("cross_sum", "zero")
         nc.vector.tensor_reduce(sq_sum[:], paged(sq[:]), AX.X, ALU.add)
         nc.vector.tensor_reduce(cross_sum[:], paged(cross[:]), AX.X, ALU.add)
         r, r2 = small("r", "v_pool3_0"), small("r2")
@@ -183,7 +186,6 @@ def tile_attend_ttpagestandard_kernel(tc, query, keys_words, keys_scales, dquery
         warm_exp = column("warm_exp")
         nc.scalar.activation(warm_exp[:], r2[:, 0:1], ACT.Exp, scale=-1.0)
 
-        gather_values(1, "rounded0")
         k = small("k")
         nc.vector.tensor_tensor(k[:], cross_sum[:], r2[:], ALU.mult)
         s = big("s")
@@ -199,7 +201,7 @@ def tile_attend_ttpagestandard_kernel(tc, query, keys_words, keys_scales, dquery
         nc.scalar.activation(p[:], s[:], ACT.Exp, bias=neg_max[:], accum_out=z[:])
         gather_values(3, "picked3")
         ts = big("ts")
-        nc.vector.tensor_tensor(ts[:], x[:], y[:], ALU.subtract)
+        nc.gpsimd.tensor_tensor(ts[:], x[:], y[:], ALU.subtract)
         gather_values(2, "ce")
 
         v_grouped = [

@@ -54,26 +54,27 @@ def tile_attend_ttpagestandard_kernel(tc, query, keys_words, keys_scales, dquery
             nc.sync.dma_start(raw[:], src.rearrange("(p j) w -> p j w", j=PACK))
             return raw
 
-        q_raw = load_rows(query, "q_raw")
         kw_pool = sb.tile([P, T], U16, name="kw_pool", align_bytes=64)
         nc.sync.dma_start(kw_pool[:].bitcast(I32), keys_words[0].bitcast(I32))
+        os_cols = sb.tile([P, PACK], F32, name="os_cols")
+        nc.sync.dma_start(os_cols[:], slot_factor.rearrange("o (p t) -> (o p) t", t=PACK))
+        q_raw = load_rows(query, "q_raw")
         dq_raw = load_rows(dquery, "dq_raw")
         v_pool = {}
 
-        def load_values(b, part, parts):
-            width = T // parts
-            name = "v_pool%d_%d" % (b, part)
-            v_pool[b, part] = sb.tile([P, width], F32, name=name, tag=name, align_bytes=64)
-            nc.sync.dma_start(v_pool[b, part][:], vals[b * P : (b + 1) * P, part * width : (part + 1) * width])
+        def load_values(b, c0, c1):
+            name = "v_pool%d_%d" % (b, c0)
+            v_pool[b, c0] = sb.tile([P, c1 - c0], F32, name=name, tag=name, align_bytes=64)
+            nc.sync.dma_start(v_pool[b, c0][:], vals[b * P : (b + 1) * P, c0:c1])
 
-        load_values(0, 0, 2)
-        load_values(0, 1, 2)
-        load_values(1, 0, 1)
-        os_cols = sb.tile([P, PACK], F32, name="os_cols", tag="os_cols", align_bytes=64)
-        nc.sync.dma_start(os_cols[:], slot_factor.rearrange("o (p t) -> (o p) t", t=PACK))
-        load_values(3, 0, 2)
-        load_values(2, 0, 1)
-        load_values(3, 1, 2)
+        load_values(0, 0, 1024)
+        load_values(0, 1024, 2048)
+        load_values(1, 0, T)
+        load_values(3, 0, 512)
+        load_values(3, 512, 1024)
+        load_values(2, 0, T)
+        load_values(3, 1024, 1536)
+        load_values(3, 1536, 2048)
 
         ident = sb.tile([P, P], F32, name="ident")
         make_identity(nc, ident[:])
@@ -81,28 +82,28 @@ def tile_attend_ttpagestandard_kernel(tc, query, keys_words, keys_scales, dquery
         warm_in = sb.tile([P, 1], F32, name="warm_in")
         warm_out = sb.tile([P, 1], F32, name="warm_out")
         nc.gpsimd.memset(warm_in[:], 1.0)
-        zero = sb.tile([P, 1], F32, name="zero", tag="zero", align_bytes=64)
-        nc.gpsimd.memset(zero[:], 0.0)
         nc.scalar.activation(warm_out[:], warm_in[:], ACT.Abs_reciprocal_sqrt)
 
-        ks = sb.tile([P, I], U8, name="ks", align_bytes=64)
-        nc.vector.tensor_copy(ks[:], ks_pool[:].indirect(offsets[:]))
-
-        def quantize_rows(raw, name):
+        def quantize_rows(raw, name, copy):
             grouped = sb.tile([P, Q * PACK], BF16, name=name + "_grouped", align_bytes=64)
-            nc.scalar.copy(grouped[:].rearrange("p (w j) -> p w j", j=PACK), raw[:].rearrange("p j w -> p w j"))
+            copy(grouped[:].rearrange("p (w j) -> p w j", j=PACK), raw[:].rearrange("p j w -> p w j"))
             codes = sb.tile([P, Q], U32, name=name + "_codes", align_bytes=64)
             scales = sb.tile([P, Q], U8, name=name + "_scales", align_bytes=64)
             nc.vector.quantize_mx(out=codes[:].bitcast(FP8X4), scales=scales[:], in_=grouped[:])
             return codes, scales
 
-        q_mx = quantize_rows(q_raw, "q")
-        kw = []
-        for h in range(2):
-            half = sb.tile([P, I // 2], U16, name="kw%d" % h, align_bytes=64)
-            nc.vector.tensor_copy(half[:], kw_pool[:].indirect(offsets[:, 16 * h : 16 * (h + 1)]))
-            kw.append(half)
-        dq_mx = quantize_rows(dq_raw, "dq")
+        def gather_keys(pool_tile, dtype, name):
+            halves = []
+            for h in range(2):
+                half = sb.tile([P, I // 2], dtype, name="%s%d" % (name, h), align_bytes=64)
+                nc.vector.tensor_copy(half[:], pool_tile[:].indirect(offsets[:, 16 * h : 16 * (h + 1)]))
+                halves.append(half)
+            return halves
+
+        q_mx = quantize_rows(q_raw, "q", nc.scalar.copy)
+        kw = gather_keys(kw_pool, U16, "kw")
+        ks = gather_keys(ks_pool, U8, "ks")
+        dq_mx = quantize_rows(dq_raw, "dq", nc.scalar.copy)
 
         scores = []
         for n, (codes, scales) in enumerate((q_mx, dq_mx)):
@@ -114,7 +115,7 @@ def tile_attend_ttpagestandard_kernel(tc, query, keys_words, keys_scales, dquery
                     lhsT=codes[:].bitcast(FP8X4),
                     lhsT_scale=scales[:],
                     rhs=kw[h][:].bitcast(FP4X4),
-                    rhs_scale=ks[:, cols],
+                    rhs_scale=ks[h][:],
                     start=True,
                     stop=True,
                 )
@@ -135,12 +136,11 @@ def tile_attend_ttpagestandard_kernel(tc, query, keys_words, keys_scales, dquery
         rounded = {}
         picked = {}
 
-        def round_values(b, part):
-            if part == 0:
+        def round_values(b, c0, c1):
+            if c0 == 0:
                 rounded[b] = sb.tile([P, T], BF16, name="rounded%d" % b, tag="rounded%d" % b, align_bytes=64)
-            for c in range(0, T // 2, CAST_COLS):
-                c0 = part * T // 2 + c
-                nc.scalar.activation(rounded[b][:, c0 : c0 + CAST_COLS], v_pool[b, part][:, c : c + CAST_COLS], ACT.Copy)
+            for c in range(c0, c1, CAST_COLS):
+                nc.scalar.activation(rounded[b][:, c : c + CAST_COLS], v_pool[b, c0][:, c - c0 : c - c0 + CAST_COLS], ACT.Copy)
 
         def gather_values(b, tag):
             picked[b] = sb.tile([P, I], BF16, name="picked%d" % b, tag=tag, align_bytes=64)
@@ -151,7 +151,7 @@ def tile_attend_ttpagestandard_kernel(tc, query, keys_words, keys_scales, dquery
 
         def turn_values(b):
             words = picked[b][:].bitcast(F32)
-            turn([words[:, u : 2 * P : 2] for u in range(2)], v_grouped[b // 2][:].bitcast(F32)[:, 2 * P * (b % 2) : 2 * P * (b % 2 + 1)], "turn%d" % b, nc.scalar.copy)
+            turn([words[:, u : 2 * P : 2] for u in range(2)], v_words[b // 2][:, 2 * P * (b % 2) : 2 * P * (b % 2 + 1)], "turn%d" % b, nc.scalar.copy)
 
         def big(name, tag=None):
             return sb.tile([P, I], F32, name=name, tag=tag or name, align_bytes=64)
@@ -168,54 +168,57 @@ def tile_attend_ttpagestandard_kernel(tc, query, keys_words, keys_scales, dquery
         ce, tce = big("ce"), big("tce")
         nc.vector.scalar_tensor_tensor(paged(ce[:]), per_slot(a_sum[:]), -1.0 / PAGE, paged(a[:]), ALU.mult, ALU.add)
         nc.vector.scalar_tensor_tensor(paged(tce[:]), per_slot(ta_sum[:]), -1.0 / PAGE, paged(ta[:]), ALU.mult, ALU.add)
-        round_values(0, 0)
-        round_values(0, 1)
+        sq = big("sq")
+        nc.gpsimd.tensor_tensor(sq[:], ce[:], ce[:], ALU.mult)
+        cross = big("cross")
+        nc.vector.tensor_tensor(cross[:], ta[:], ce[:], ALU.mult)
+        round_values(0, 0, 1024)
+        round_values(0, 1024, 2048)
         gather_values(0, "picked0")
         gather_values(1, "picked1")
-        sq = big("sq", "os_cols")
-        nc.scalar.activation(sq[:], ce[:], ACT.Square, bias=zero[:])
-        round_values(3, 0)
-        cross = big("cross")
-        nc.gpsimd.tensor_tensor(cross[:], tce[:], ce[:], ALU.mult)
-        sq_sum, cross_sum = small("sq_sum"), small("cross_sum", "zero")
+        round_values(3, 0, 512)
+        round_values(3, 512, 1024)
+        sq_sum = small("sq_sum", "v_pool3_0")
+        shared = sb.tile([P, G + 2 * OUT_COLS], F32, name="shared", tag="v_pool3_512", align_bytes=64)
+        cross_sum = shared[:, :G]
+        v_words = [shared[:, G:]]
         nc.vector.tensor_reduce(sq_sum[:], paged(sq[:]), AX.X, ALU.add)
-        nc.vector.tensor_reduce(cross_sum[:], paged(cross[:]), AX.X, ALU.add)
-        r, r2 = small("r", "v_pool3_0"), small("r2")
+        nc.vector.tensor_reduce(cross_sum, paged(cross[:]), AX.X, ALU.add)
+        r = small("r")
         nc.scalar.activation(r[:], sq_sum[:], ACT.Abs_reciprocal_sqrt, bias=0.3, scale=1.0 / PAGE)
-        nc.scalar.activation(r2[:], r[:], ACT.Square, scale=0.25)
         warm_exp = column("warm_exp")
-        nc.scalar.activation(warm_exp[:], r2[:, 0:1], ACT.Exp, scale=-1.0)
+        nc.scalar.activation(warm_exp[:], r[:, 0:1], ACT.Exp, scale=-1.0)
 
-        k = small("k")
-        nc.vector.tensor_tensor(k[:], cross_sum[:], r2[:], ALU.mult)
         s = big("s")
         nc.vector.tensor_tensor(paged(s[:]), paged(ce[:]), per_slot(r[:]), ALU.mult)
+        kr, k = small("kr"), small("k")
+        nc.vector.scalar_tensor_tensor(kr[:], cross_sum, 1.0 / PAGE, r[:], ALU.mult, ALU.mult)
         x = big("x")
         nc.vector.tensor_tensor(paged(x[:]), paged(tce[:]), per_slot(r[:]), ALU.mult)
-        y = big("y")
-        nc.vector.tensor_tensor(paged(y[:]), paged(s[:]), per_slot(k[:]), ALU.mult)
+        nc.vector.tensor_tensor(k[:], kr[:], r[:], ALU.mult)
         neg_max = column("neg_max")
         nc.vector.tensor_reduce(neg_max[:], s[:], AX.X, ALU.max, negate=True)
-        round_values(3, 1)
-        p, z = big("p", "v_pool3_1"), column("z")
+        y = big("y")
+        nc.gpsimd.tensor_tensor(paged(y[:]), paged(s[:]), per_slot(k[:]), ALU.mult)
+        round_values(3, 1024, 1536)
+        p, z = big("p", "v_pool3_1024"), column("z")
         nc.scalar.activation(p[:], s[:], ACT.Exp, bias=neg_max[:], accum_out=z[:])
+        round_values(3, 1536, 2048)
         gather_values(3, "picked3")
-        ts = big("ts")
-        nc.gpsimd.tensor_tensor(ts[:], x[:], y[:], ALU.subtract)
         gather_values(2, "ce")
+        ts = big("ts")
+        nc.vector.tensor_tensor(ts[:], x[:], y[:], ALU.subtract)
 
-        v_grouped = [
-            sb.tile([P, OUT_COLS * PACK], BF16, name="v_grouped%d" % h, tag=("sq_sum", "v_grouped1")[h], align_bytes=64)
-            for h in range(2)
-        ]
-        for b in (0, 1, 2, 3):
+        v_words1 = sb.tile([P, 2 * OUT_COLS], F32, name="v_words1", tag="s", align_bytes=64)
+        v_words.append(v_words1[:])
+        for b in range(E_BLOCKS):
             turn_values(b)
         v_mx = []
 
         def quantize_values(h, tag):
             v_codes = sb.tile([P, OUT_COLS], U32, name="v_codes%d" % h, tag=tag, align_bytes=64)
             v_scales = sb.tile([P, OUT_COLS], U8, name="v_scales%d" % h, align_bytes=64)
-            nc.vector.quantize_mx(out=v_codes[:].bitcast(FP8X4), scales=v_scales[:], in_=v_grouped[h][:])
+            nc.vector.quantize_mx(out=v_codes[:].bitcast(FP8X4), scales=v_scales[:], in_=v_words[h].bitcast(BF16))
             v_mx.append((v_codes, v_scales))
 
         rz = column("rz")
@@ -235,7 +238,7 @@ def tile_attend_ttpagestandard_kernel(tc, query, keys_words, keys_scales, dquery
         quantize_values(0, "tp")
         w = []
         for u in range(2):
-            part = sb.tile([P, P, 2], BF16, name="w%d" % u, align_bytes=64)
+            part = sb.tile([P, P, 2], BF16, name="w%d" % u, tag="w%d" % u, align_bytes=64)
             nc.vector.scalar_tensor_tensor(
                 part[:],
                 ts[:].rearrange("p (n t) -> p n t", t=PACK)[:, :, 2 * u : 2 * u + 2],
@@ -251,7 +254,7 @@ def tile_attend_ttpagestandard_kernel(tc, query, keys_words, keys_scales, dquery
         w_scales = sb.tile([P, Q], U8, name="w_scales", align_bytes=64)
         nc.vector.quantize_mx(out=w_codes[:].bitcast(FP8X4), scales=w_scales[:], in_=w_grouped[:])
 
-        quantize_values(1, "pos")
+        quantize_values(1, "w1")
 
         for h in range(E // OUT_COLS):
             cols = slice(h * OUT_COLS, (h + 1) * OUT_COLS)

@@ -42,12 +42,7 @@ def tile_attend_ttpagestandard_kernel(tc, query, keys_words, keys_scales, dquery
         offsets = sb.tile([P, I // 16], U16, name="offsets")
         nc.sync.dma_start(offsets[:], offs)
         ks_pool = sb.tile([P, T], U8, name="ks_pool", align_bytes=64)
-        nc.gpsimd.memset(ks_pool[:].bitcast(I32), 0)
-        for quad in range(4):
-            nc.scalar.dma_start(
-                ks_pool[32 * quad : 32 * quad + 4, :].bitcast(I32),
-                keys_scales[0, 4 * quad : 4 * quad + 4, :].bitcast(I32),
-            )
+        nc.vector.memset(ks_pool[:].bitcast(I32), 0)
 
         def load_rows(src, name):
             raw = sb.tile([P, PACK, Q], F32, name=name)
@@ -56,8 +51,11 @@ def tile_attend_ttpagestandard_kernel(tc, query, keys_words, keys_scales, dquery
 
         kw_pool = sb.tile([P, T], U16, name="kw_pool", align_bytes=64)
         nc.sync.dma_start(kw_pool[:].bitcast(I32), keys_words[0].bitcast(I32))
-        os_cols = sb.tile([P, PACK], F32, name="os_cols")
-        nc.sync.dma_start(os_cols[:], slot_factor.rearrange("o (p t) -> (o p) t", t=PACK))
+        for quad in range(4):
+            nc.sync.dma_start(
+                ks_pool[32 * quad : 32 * quad + 4, :].bitcast(I32),
+                keys_scales[0, 4 * quad : 4 * quad + 4, :].bitcast(I32),
+            )
         q_raw = load_rows(query, "q_raw")
         dq_raw = load_rows(dquery, "dq_raw")
         v_pool = {}
@@ -67,8 +65,10 @@ def tile_attend_ttpagestandard_kernel(tc, query, keys_words, keys_scales, dquery
             v_pool[b, c0] = sb.tile([P, c1 - c0], F32, name=name, tag=name, align_bytes=64)
             nc.sync.dma_start(v_pool[b, c0][:], vals[b * P : (b + 1) * P, c0:c1])
 
-        load_values(0, 0, 1024)
-        load_values(0, 1024, 2048)
+        for c in range(0, T, CAST_COLS):
+            load_values(0, c, c + CAST_COLS)
+        os_cols = sb.tile([P, PACK], F32, name="os_cols")
+        nc.sync.dma_start(os_cols[:], slot_factor.rearrange("o (p t) -> (o p) t", t=PACK))
         load_values(1, 0, T)
         load_values(3, 0, 512)
         load_values(3, 512, 1024)
@@ -172,8 +172,8 @@ def tile_attend_ttpagestandard_kernel(tc, query, keys_words, keys_scales, dquery
         nc.gpsimd.tensor_tensor(sq[:], ce[:], ce[:], ALU.mult)
         cross = big("cross")
         nc.vector.tensor_tensor(cross[:], ta[:], ce[:], ALU.mult)
-        round_values(0, 0, 1024)
-        round_values(0, 1024, 2048)
+        for c in range(0, T, CAST_COLS):
+            round_values(0, c, c + CAST_COLS)
         gather_values(0, "picked0")
         gather_values(1, "picked1")
         round_values(3, 0, 512)

from contextlib import ExitStack

import concourse.mybir as mybir
from concourse.masks import make_identity

D, E, T, I, Q, G = 512, 512, 2048, 512, 128, 32
FLOPS = 2 * Q * I * (2 * D + E)

F32 = mybir.dt.float32
BF16 = mybir.dt.bfloat16
I32 = mybir.dt.int32
U32 = mybir.dt.uint32
U16 = mybir.dt.uint16
U8 = mybir.dt.uint8
FP8X4 = mybir.dt.float8_e4m3fn_x4
FP4X4 = mybir.dt.float4_e2m1fn_x4
ALU = mybir.AluOpType
ACT = mybir.ActivationFunctionType
AX = mybir.AxisListType

P = 128
PACK = 4
PAGE = I // G
E_BLOCKS = E // P
SCALAR_BLOCKS = (0, 3)
CAST_COLS = 512
OUT_COLS = 256


def tile_attend_ttpagestandard_kernel(tc, query, keys_words, keys_scales, dquery, slot_factor, vals, offs, out):
    nc = tc.nc
    with ExitStack() as ctx:
        sb = ctx.enter_context(tc.tile_pool(name="sb", bufs=1))
        ps = ctx.enter_context(tc.psum_pool(name="ps", bufs=1))

        def paged(ap):
            return ap.rearrange("p (g j) -> p g j", j=PAGE)

        def per_slot(ap):
            return ap.unsqueeze(2).to_broadcast([P, G, PAGE])

        offsets = sb.tile([P, I // 16], U16, name="offsets")
        nc.sync.dma_start(offsets[:], offs)
        ks_pool = sb.tile([P, T], U8, name="ks_pool", align_bytes=64)
        nc.vector.memset(ks_pool[:].bitcast(I32), 0)

        def load_rows(src, name):
            raw = sb.tile([P, PACK, Q], F32, name=name)
            nc.sync.dma_start(raw[:], src.rearrange("(p j) w -> p j w", j=PACK))
            return raw

        kw_pool = sb.tile([P, T], U16, name="kw_pool", align_bytes=64)
        nc.sync.dma_start(kw_pool[:].bitcast(I32), keys_words[0].bitcast(I32))
        for quad in range(4):
            nc.sync.dma_start(
                ks_pool[32 * quad : 32 * quad + 4, :].bitcast(I32),
                keys_scales[0, 4 * quad : 4 * quad + 4, :].bitcast(I32),
            )
        q_raw = load_rows(query, "q_raw")
        dq_raw = load_rows(dquery, "dq_raw")
        v_pool = {}

        def load_values(b, c0, c1):
            name = "v_pool%d_%d" % (b, c0)
            v_pool[b, c0] = sb.tile([P, c1 - c0], F32, name=name, tag=name, align_bytes=64)
            nc.sync.dma_start(v_pool[b, c0][:], vals[b * P : (b + 1) * P, c0:c1])

        for c in range(0, T, CAST_COLS):
            load_values(0, c, c + CAST_COLS)
        os_cols = sb.tile([P, PACK], F32, name="os_cols")
        nc.sync.dma_start(os_cols[:], slot_factor.rearrange("o (p t) -> (o p) t", t=PACK))
        load_values(1, 0, T)
        load_values(3, 0, 512)
        load_values(3, 512, 1024)
        load_values(2, 0, T)
        load_values(3, 1024, 1536)
        load_values(3, 1536, 2048)

        ident = sb.tile([P, P], F32, name="ident")
        make_identity(nc, ident[:])

        warm_in = sb.tile([P, 1], F32, name="warm_in")
        warm_out = sb.tile([P, 1], F32, name="warm_out")
        nc.gpsimd.memset(warm_in[:], 1.0)
        nc.scalar.activation(warm_out[:], warm_in[:], ACT.Abs_reciprocal_sqrt)

        def quantize_rows(raw, name, copy):
            grouped = sb.tile([P, Q * PACK], BF16, name=name + "_grouped", align_bytes=64)
            copy(grouped[:].rearrange("p (w j) -> p w j", j=PACK), raw[:].rearrange("p j w -> p w j"))
            codes = sb.tile([P, Q], U32, name=name + "_codes", align_bytes=64)
            scales = sb.tile([P, Q], U8, name=name + "_scales", align_bytes=64)
            nc.vector.quantize_mx(out=codes[:].bitcast(FP8X4), scales=scales[:], in_=grouped[:])
            return codes, scales

        def gather_keys(pool_tile, dtype, name):
            halves = []
            for h in range(2):
                half = sb.tile([P, I // 2], dtype, name="%s%d" % (name, h), align_bytes=64)
                nc.vector.tensor_copy(half[:], pool_tile[:].indirect(offsets[:, 16 * h : 16 * (h + 1)]))
                halves.append(half)
            return halves

        q_mx = quantize_rows(q_raw, "q", nc.scalar.copy)
        kw = gather_keys(kw_pool, U16, "kw")
        ks = gather_keys(ks_pool, U8, "ks")
        dq_mx = quantize_rows(dq_raw, "dq", nc.scalar.copy)

        scores = []
        for n, (codes, scales) in enumerate((q_mx, dq_mx)):
            bank = ps.tile([P, I], F32, name="scores%d" % n)
            for h in range(2):
                cols = slice(h * I // 2, (h + 1) * I // 2)
                nc.tensor.matmul_mx(
                    out=bank[:, cols],
                    lhsT=codes[:].bitcast(FP8X4),
                    lhsT_scale=scales[:],
                    rhs=kw[h][:].bitcast(FP4X4),
                    rhs_scale=ks[h][:],
                    start=True,
                    stop=True,
                )
            scores.append(bank)
        a, ta = scores

        os_bank = ps.tile([P, PACK, P], F32, name="os_bank")
        for t in range(PACK):
            nc.tensor.transpose(os_bank[:, t, :], os_cols[:, t : t + 1].to_broadcast([P, P]), ident[:])


        def turn(word_sets, dst_words, tag, copy):
            bank = ps.tile([P, 2, P], F32, name=tag, tag=tag)
            for u in range(2):
                nc.tensor.transpose(bank[:, u, :], word_sets[u], ident[:])
            copy(dst_words.rearrange("p (r u) -> p r u", u=2), bank[:].rearrange("p u r -> p r u"))

        rounded = {}
        picked = {}

        def round_values(b, c0, c1):
            if c0 == 0:
                rounded[b] = sb.tile([P, T], BF16, name="rounded%d" % b, tag="rounded%d" % b, align_bytes=64)
            for c in range(c0, c1, CAST_COLS):
                nc.scalar.activation(rounded[b][:, c : c + CAST_COLS], v_pool[b, c0][:, c - c0 : c - c0 + CAST_COLS], ACT.Copy)

        def gather_values(b, tag):
            picked[b] = sb.tile([P, I], BF16, name="picked%d" % b, tag=tag, align_bytes=64)
            if b in SCALAR_BLOCKS:
                nc.scalar.activation(picked[b][:], rounded[b][:].indirect(offsets[:]), ACT.Copy)
            else:
                nc.vector.tensor_copy(picked[b][:], v_pool[b, 0][:].indirect(offsets[:]))

        def turn_values(b):
            words = picked[b][:].bitcast(F32)
            turn([words[:, u : 2 * P : 2] for u in range(2)], v_words[b // 2][:, 2 * P * (b % 2) : 2 * P * (b % 2 + 1)], "turn%d" % b, nc.scalar.copy)

        def big(name, tag=None):
            return sb.tile([P, I], F32, name=name, tag=tag or name, align_bytes=64)

        def small(name, tag=None):
            return sb.tile([P, G], F32, name=name, tag=tag or name, align_bytes=64)

        def column(name):
            return sb.tile([P, 1], F32, name=name)

        a_sum, ta_sum = small("a_sum"), small("ta_sum")
        nc.vector.tensor_reduce(a_sum[:], paged(a[:]), AX.X, ALU.add)
        nc.vector.tensor_reduce(ta_sum[:], paged(ta[:]), AX.X, ALU.add)
        ce, tce = big("ce"), big("tce")
        nc.vector.scalar_tensor_tensor(paged(ce[:]), per_slot(a_sum[:]), -1.0 / PAGE, paged(a[:]), ALU.mult, ALU.add)
        nc.vector.scalar_tensor_tensor(paged(tce[:]), per_slot(ta_sum[:]), -1.0 / PAGE, paged(ta[:]), ALU.mult, ALU.add)
        sq = big("sq")
        nc.gpsimd.tensor_tensor(sq[:], ce[:], ce[:], ALU.mult)
        cross = big("cross")
        nc.vector.tensor_tensor(cross[:], ta[:], ce[:], ALU.mult)
        for c in range(0, T, CAST_COLS):
            round_values(0, c, c + CAST_COLS)
        gather_values(0, "picked0")
        gather_values(1, "picked1")
        round_values(3, 0, 512)
        round_values(3, 512, 1024)
        sq_sum = small("sq_sum", "v_pool3_0")
        shared = sb.tile([P, G + 2 * OUT_COLS], F32, name="shared", tag="v_pool3_512", align_bytes=64)
        cross_sum = shared[:, :G]
        v_words = [shared[:, G:]]
        nc.vector.tensor_reduce(sq_sum[:], paged(sq[:]), AX.X, ALU.add)
        nc.vector.tensor_reduce(cross_sum, paged(cross[:]), AX.X, ALU.add)
        r = small("r")
        nc.scalar.activation(r[:], sq_sum[:], ACT.Abs_reciprocal_sqrt, bias=0.3, scale=1.0 / PAGE)
        warm_exp = column("warm_exp")
        nc.scalar.activation(warm_exp[:], r[:, 0:1], ACT.Exp, scale=-1.0)

        s = big("s")
        nc.vector.tensor_tensor(paged(s[:]), paged(ce[:]), per_slot(r[:]), ALU.mult)
        kr, k = small("kr"), small("k")
        nc.vector.scalar_tensor_tensor(kr[:], cross_sum, 1.0 / PAGE, r[:], ALU.mult, ALU.mult)
        x = big("x")
        nc.vector.tensor_tensor(paged(x[:]), paged(tce[:]), per_slot(r[:]), ALU.mult)
        nc.vector.tensor_tensor(k[:], kr[:], r[:], ALU.mult)
        neg_max = column("neg_max")
        nc.vector.tensor_reduce(neg_max[:], s[:], AX.X, ALU.max, negate=True)
        y = big("y")
        nc.gpsimd.tensor_tensor(paged(y[:]), paged(s[:]), per_slot(k[:]), ALU.mult)
        round_values(3, 1024, 1536)
        p, z = big("p", "v_pool3_1024"), column("z")
        nc.scalar.activation(p[:], s[:], ACT.Exp, bias=neg_max[:], accum_out=z[:])
        round_values(3, 1536, 2048)
        gather_values(3, "picked3")
        gather_values(2, "ce")
        ts = big("ts")
        nc.vector.tensor_tensor(ts[:], x[:], y[:], ALU.subtract)

        v_words1 = sb.tile([P, 2 * OUT_COLS], F32, name="v_words1", tag="s", align_bytes=64)
        v_words.append(v_words1[:])
        for b in range(E_BLOCKS):
            turn_values(b)
        v_mx = []

        def quantize_values(h, tag):
            v_codes = sb.tile([P, OUT_COLS], U32, name="v_codes%d" % h, tag=tag, align_bytes=64)
            v_scales = sb.tile([P, OUT_COLS], U8, name="v_scales%d" % h, align_bytes=64)
            nc.vector.quantize_mx(out=v_codes[:].bitcast(FP8X4), scales=v_scales[:], in_=v_words[h].bitcast(BF16))
            v_mx.append((v_codes, v_scales))

        rz = column("rz")
        nc.vector.reciprocal(rz[:], z[:])
        tp, tz, tau = big("tp"), column("tz"), column("tau")
        nc.vector.scalar_tensor_tensor(tp[:], p[:], 1.0, ts[:], ALU.mult, ALU.mult, accum_out=tz[:])
        pos = big("pos")
        nc.vector.scalar_tensor_tensor(
            pos[:].rearrange("p (n t) -> p n t", t=PACK),
            p[:].rearrange("p (n t) -> p n t", t=PACK),
            rz[:],
            os_bank[:].rearrange("p t n -> p n t"),
            ALU.mult,
            ALU.mult,
        )
        nc.vector.tensor_tensor(tau[:], tz[:], rz[:], ALU.mult)
        quantize_values(0, "tp")
        w = []
        for u in range(2):
            part = sb.tile([P, P, 2], BF16, name="w%d" % u, tag="w%d" % u, align_bytes=64)
            nc.vector.scalar_tensor_tensor(
                part[:],
                ts[:].rearrange("p (n t) -> p n t", t=PACK)[:, :, 2 * u : 2 * u + 2],
                tau[:],
                pos[:].rearrange("p (n t) -> p n t", t=PACK)[:, :, 2 * u : 2 * u + 2],
                ALU.subtract,
                ALU.mult,
            )
            w.append(part[:].rearrange("p n e -> p (n e)").bitcast(F32))
        w_grouped = sb.tile([P, Q * PACK], BF16, name="w_grouped", align_bytes=64)
        turn(w, w_grouped[:].bitcast(F32), "turn_w", nc.vector.tensor_copy)
        w_codes = sb.tile([P, Q], U32, name="w_codes", align_bytes=64)
        w_scales = sb.tile([P, Q], U8, name="w_scales", align_bytes=64)
        nc.vector.quantize_mx(out=w_codes[:].bitcast(FP8X4), scales=w_scales[:], in_=w_grouped[:])

        quantize_values(1, "w1")

        for h in range(E // OUT_COLS):
            cols = slice(h * OUT_COLS, (h + 1) * OUT_COLS)
            acc = ps.tile([P, OUT_COLS], F32, name="acc%d" % h, tag="scores%d" % h)
            nc.tensor.matmul_mx(
                out=acc[:],
                lhsT=w_codes[:].bitcast(FP8X4),
                lhsT_scale=w_scales[:],
                rhs=v_mx[h][0][:].bitcast(FP8X4),
                rhs_scale=v_mx[h][1][:],
                start=True,
                stop=True,
            )
            res = sb.tile([P, OUT_COLS], F32, name="res%d" % h)
            if h == 0:
                nc.scalar.copy(res[:], acc[:])
                nc.scalar.dma_start(out[:, cols], res[:])
            else:
                nc.vector.tensor_copy(res[:], acc[:])
                nc.sync.dma_start(out[:, cols], res[:])
